import numpy as np
import ml_dtypes


def mxq(x, axis, fmt="e4m3"):
    dtype, down = {"e4m3": (ml_dtypes.float8_e4m3fn, 7), "e5m2": (ml_dtypes.float8_e5m2, 14)}[fmt]
    v = np.moveaxis(np.asarray(x, np.float32).astype(ml_dtypes.bfloat16).astype(np.float64), axis, -1)
    blocks = v.reshape(v.shape[:-1] + (-1, 32))
    amax = np.abs(blocks).max(-1, keepdims=True)
    byte = np.maximum(np.where(amax > 0, np.frexp(amax)[1] - 1 + 127, 0) - down, 1)
    scale = np.exp2(byte - 127.0)
    codes = (blocks / scale).astype(np.float32).astype(dtype).astype(np.float64)
    return np.moveaxis((codes * scale).reshape(v.shape), -1, axis)


WIDE = False


def mx_kscale(k):
    if not WIDE:
        return np.ones(k)
    levels = np.array([10, -10, 5, -5, 0])
    if k % 512:
        return np.exp2(np.random.permutation(np.resize(levels, k // 32))).repeat(32)
    a = np.empty((k // 512, 16))
    for p in range(k // 512):
        a[p, :8] = np.random.permutation(np.resize(levels, 8))
        for g in range(8):
            far = levels[np.abs(levels - a[p, g]) >= 10]
            a[p, g + 8] = far[np.random.randint(len(far))]
    return np.exp2(a.ravel()).repeat(32)


def f64(x):
    return np.asarray(x).astype(np.float64)


def striped(idx):
    return np.tile(idx.reshape(-1, 16).T, (8, 1)).astype(np.uint16)


def unstriped(offs):
    return offs[:16].T.reshape(-1).astype(np.int64)


def striped8(idx):
    return np.concatenate([x.reshape(-1, 16).T for x in idx]).astype(np.uint16)


def runs(offs, k):
    lists = np.stack([offs[16 * r : 16 * r + 16].T.reshape(-1) for r in range(8)]).astype(np.int64)
    return lists[np.arange(k) % 512 // 64]


def pack_weight(w):
    k, n = w.shape
    w = f64(np.asarray(w, np.float32).astype(ml_dtypes.bfloat16)).reshape(k // 32, 32, n)
    amax = np.abs(w).max(1)
    byte = np.clip(np.where(amax > 0, np.frexp(amax)[1] - 1 + 127 - 7, 1), 1, 254)
    scaled = (w * np.exp2(127.0 - byte)[:, None, :]).reshape(k, n).astype(np.float32)
    words = np.ascontiguousarray(scaled.reshape(k // 512, 128, 4, n).transpose(0, 1, 3, 2)).astype(ml_dtypes.float8_e4m3fn).view(np.uint8)
    return words, np.ascontiguousarray(byte.astype(np.uint8).reshape(k // 512, 16, n))


def unpack_weight(words, scales):
    g, p, n, _ = words.shape
    vals = np.ascontiguousarray(words).view(ml_dtypes.float8_e4m3fn).astype(np.float64) * np.repeat(np.exp2(scales.astype(np.float64) - 127.0), 8, axis=1)[..., None]
    return vals.transpose(0, 1, 3, 2).reshape(g * 512, n)


def sigmoid(v):
    return 1.0 / (1.0 + np.exp(-np.maximum(v, -700.0)))


K, T, S, V, H = 512, 2048, 512, 256, 512


def setup_inputs():
    n = np.random.standard_normal
    s = mx_kscale(K)[:, None]
    u = mx_kscale(S)
    packed_xT = pack_weight(n((K, T)) * s)
    return {
        "x_words": packed_xT[0],
        "x_scales": packed_xT[1],
        "w1": (n((K, H)) / np.sqrt(K) / s).astype(np.float32),
        "w2": (n((K, H)) / np.sqrt(K) / s).astype(np.float32),
        "w3": (n((K, H)) / np.sqrt(K) / s).astype(np.float32),
        "ga": (np.random.uniform(0.5, 1.5, (H, 1)) * u[:, None]).astype(np.float32),
        "gb": (np.random.uniform(0.5, 1.5, (H, 1)) / u[:, None]).astype(np.float32),
        "offs": striped(np.random.permutation(T)[:S]),
        "two": striped(np.random.permutation(T)[:S]),
        "n1": striped(np.random.permutation(S)),
        "n2": striped(np.random.permutation(S)),
        "three": striped(np.random.permutation(T)[:V]),
        "n3": striped8(np.stack([np.random.permutation(V) for _ in range(8)])),
        "n4": striped8(np.stack([np.random.permutation(V) for _ in range(8)])),
        "n5": striped8(np.stack([np.random.permutation(V) for _ in range(8)])),
    }


def reference(x_words, x_scales, w1, w2, w3, ga, gb, offs, two, n1, n2, three, n3, n4, n5):
    xq = unpack_weight(x_words, x_scales)[:, unstriped(offs)]
    y = mxq(f64(w1), 0, "e4m3").T @ xq
    x_two = unpack_weight(x_words, x_scales)[:, unstriped(two)]
    d = mxq(f64(w2), 0, "e4m3").T @ x_two
    z = f64(ga) * ((y + y[:, unstriped(n1)]) * (sigmoid(d + d[:, unstriped(n2)])))
    x_three = unpack_weight(x_words, x_scales)[:, unstriped(three)]
    b = mxq(f64(w3), 0, "e4m3").T @ x_three
    z2 = f64(gb) * (np.maximum(b, b[np.arange(H)[:, None], runs(n3, H)]))
    s = 0.0625 * ((mxq(z, 0, "e4m3").T @ mxq(z2, 0, "e4m3")))
    pa = s[np.arange(S)[:, None], runs(n4, S)]
    pb = s[np.arange(S)[:, None], runs(n5, S)]
    mu = 0.3125 * (s + pa + pb)
    return (s - mu) / (np.sqrt((pa - mu) ** 2 + (pb - mu) ** 2 + 0.25))

@@ -1,0 +1,263 @@
+import math
+from contextlib import ExitStack
+
+import concourse.mybir as mybir
+
+K, T, S, V, H = 512, 2048, 512, 256, 512
+FLOPS = 2 * K * H * (2 * S + V) + 2 * H * S * V
+
+F32 = mybir.dt.float32
+BF16 = mybir.dt.bfloat16
+I32 = mybir.dt.int32
+U32 = mybir.dt.uint32
+U16 = mybir.dt.uint16
+U8 = mybir.dt.uint8
+FP8X4 = mybir.dt.float8_e4m3fn_x4
+ALU = mybir.AluOpType
+ACT = mybir.ActivationFunctionType
+
+P = 128
+PACK = 4
+KEY_WINDOW = S + 32
+QUERY_WINDOW = 2 * V
+FIRST_KEYS = 384
+CAST_ENGINES = [["scalar","scalar"],["gpsimd","gpsimd"],["gpsimd","gpsimd"]]
+EVAC_D = "ssvv"
+
+WINDOW_SCALE = 1.6
+Q_OF_U = 0.375
+N_OF_U = (0.3125 / 25.6) / (0.6875 / 16.0)
+SQUARE_SCALE = 1.0 / (25.6 * math.sqrt(2.0))
+OUT_SCALE = -0.6875 / 16.0
+
+
+def tile_picked_twktriebbigstd_none_p_kernel(
+    tc, x_words, x_scales, w1, w2, w3, ga, gb, offs, two, n1, n2, three, n3, n4, n5, out
+):
+    nc = tc.nc
+    with ExitStack() as ctx:
+        keep = ctx.enter_context(tc.tile_pool(name="keep", bufs=1))
+        reuse = ctx.enter_context(tc.tile_pool(name="reuse", bufs=1))
+        psum = ctx.enter_context(tc.psum_pool(name="psum", bufs=1))
+
+        def load_list(name, src):
+            lst = keep.tile(list(src.shape), U16, name=name)
+            nc.sync.dma_start(lst[:], src)
+            return lst
+
+        def load_half(name, w, h):
+            rows = w.rearrange("(p j) c -> p j c", j=PACK)
+            raw = keep.tile([P, PACK, H // 2], F32, name=f"{name}_raw{h}")
+            nc.sync.dma_start(raw[:], rows[:, :, h * (H // 2) : (h + 1) * (H // 2)])
+            return raw[:]
+
+        def load_gain(name, g):
+            gain = keep.tile([P, PACK], F32, name=name)
+            nc.gpsimd.dma_start(gain[:], g.rearrange("(p t) o -> p (t o)", t=PACK))
+            return gain
+
+        x_sc = keep.tile([P, T], U8, name="x_sc")
+        nc.vector.memset(x_sc[:].bitcast(I32), 0)
+        w2_all = keep.tile([P, PACK, H], F32, name="w2_raw")
+        nc.sync.dma_start(w2_all[:], w2.rearrange("(p j) c -> p j c", j=PACK))
+        w2_raw = [w2_all[:, :, : H // 2], w2_all[:, :, H // 2 :]]
+        l_two = load_list("l_two", two)
+        for q in range(4):
+            (nc.scalar if q < 2 else nc.sync).dma_start(x_sc[32 * q : 32 * q + 4, :].bitcast(I32), x_scales[0, 4 * q : 4 * q + 4, :].bitcast(I32))
+        l_offs = load_list("l_offs", offs)
+        x_w = keep.tile([P, T], U32, name="x_w")
+        nc.sync.dma_start(x_w[:].bitcast(I32), x_words[0].rearrange("p n t -> p (n t)").bitcast(I32))
+        w1_raw = [load_half("w1", w1, 0)]
+        l_n2 = load_list("l_n2", n2)
+        w1_raw.append(load_half("w1", w1, 1))
+        l_three = load_list("l_three", three)
+        w3_raw = [load_half("w3", w3, 0), load_half("w3", w3, 1)]
+        l_n1 = load_list("l_n1", n1)
+        l_n3 = load_list("l_n3", n3)
+        l_n4 = load_list("l_n4", n4)
+        l_n5 = load_list("l_n5", n5)
+
+        def windows(name, used, width):
+            tiles = []
+            for t in range(PACK):
+                win = keep.tile([P, width], F32, name=f"{name}{t}")
+                nc.gpsimd.memset(win[:, used:], 0.0)
+                tiles.append(win)
+            return tiles
+
+        d_win = windows("d_win", S, KEY_WINDOW)
+        y_win = [keep.tile([P, S], F32, name=f"y_win{t}") for t in range(PACK)]
+        b_win = windows("b_win", V, QUERY_WINDOW)
+        s_win = windows("s_win", V, QUERY_WINDOW)
+        ga_sb = load_gain("ga_sb", ga)
+        gb_sb = load_gain("gb_sb", gb)
+
+        def pick(name, lst, n):
+            sc = keep.tile([P, n], U8, name=f"{name}_sc", align_bytes=64)
+            nc.vector.tensor_copy(sc[:], x_sc[:].indirect(lst[:]))
+            return sc
+
+        def pick_words(name, lst, n):
+            wd = keep.tile([P, n], U32, name=f"{name}_w", align_bytes=64)
+            nc.vector.tensor_copy(wd[:], x_w[:].indirect(lst[:]))
+            return wd
+
+        def round_weight(name, halves, engines, offset):
+            w_bf = reuse.tile([P, PACK * H], BF16, name=f"{name}_bf", align_bytes=64, offset=offset)
+            dealt = w_bf[:].rearrange("p (t m j) -> p m j t", t=PACK, j=PACK)
+            for h, raw in enumerate(halves):
+                dst = dealt[:, h * (P // 2) : (h + 1) * (P // 2)]
+                src = raw.rearrange("p j (m t) -> p m j t", t=PACK)
+                if engines[h] == "scalar":
+                    nc.scalar.copy(dst, src)
+                elif engines[h] == "gpsimd":
+                    nc.gpsimd.tensor_scalar(dst.rearrange("p m j t -> p t m j"), src.rearrange("p m j t -> p t m j"), 1.0, 0.0, ALU.mult, ALU.add)
+                else:
+                    nc.vector.tensor_copy(dst, src)
+            return w_bf
+
+        def quantize(name, bf, words, pieces=1):
+            codes = keep.tile([P, words], U32, name=f"{name}_codes", align_bytes=64)
+            scales = keep.tile([P, words], U8, name=f"{name}_scales", align_bytes=64)
+            step = words // pieces
+            for c in range(0, words, step):
+                nc.vector.quantize_mx(out=codes[:, c : c + step].bitcast(FP8X4), scales=scales[:, c : c + step], in_=bf[:, PACK * c : PACK * (c + step)])
+            return codes, scales
+
+        def product(bank, stationary, t, moving, n):
+            acc = psum.tile([P, n], F32, name=f"bank{bank}", tag=f"bank{bank}")
+            cols = slice(t * P, (t + 1) * P)
+            nc.tensor.matmul_mx(
+                out=acc[:],
+                lhsT=stationary[0][:, cols].bitcast(FP8X4),
+                lhsT_scale=stationary[1][:, cols],
+                rhs=moving[0][:].bitcast(FP8X4),
+                rhs_scale=moving[1][:],
+                start=True,
+                stop=True,
+            )
+            return acc
+
+        def evacuate(engine, dst, acc, scale):
+            if engine == "s":
+                nc.scalar.activation(dst, acc[:], ACT.Copy, scale=scale)
+            else:
+                nc.vector.tensor_scalar(dst, acc[:], scale, None, ALU.mult)
+
+        def fetch(dst, win, lst):
+            nc.scalar.activation(dst, win[:].indirect(lst[:]), ACT.Copy)
+
+        sc_two = pick("two", l_two, S)
+        sc_offs = pick("offs", l_offs, S)
+        w2_bf = round_weight("w2", w2_raw, CAST_ENGINES[0], 12288)
+        w2_q = quantize("w2", w2_bf, H)
+        x_two = (pick_words("two", l_two, S), sc_two)
+        x_offs = (pick_words("offs", l_offs, S), sc_offs)
+
+        sign = keep.tile([P, PACK], F32, name="sign")
+        nc.gpsimd.tensor_scalar(sign[:], gb_sb[:], 0.0, 2.0, ALU.is_ge, ALU.mult)
+        nc.gpsimd.tensor_scalar(sign[:], sign[:], 1.0, -1.0, ALU.mult, ALU.add)
+        ga_signed = keep.tile([P, PACK], F32, name="ga_signed")
+        gb_abs = keep.tile([P, PACK], F32, name="gb_abs")
+        nc.gpsimd.tensor_tensor(ga_signed[:], ga_sb[:], sign[:], ALU.mult)
+        nc.gpsimd.tensor_tensor(gb_abs[:], gb_sb[:], sign[:], ALU.mult)
+        w1_bf = round_weight("w1", w1_raw, CAST_ENGINES[1], 2048)
+
+        d_acc = []
+        d_near = keep.tile([P, PACK, S], F32, name="d_near")
+        for t in range(PACK):
+            d_acc.append(product(t, w2_q, t, x_two, S))
+            evacuate(EVAC_D[t], d_win[t][:, :S], d_acc[t], 1.0)
+            fetch(d_near[:, t, :], d_win[t], l_n2)
+        x_three = (pick_words("three", l_three, V), pick("three", l_three, V))
+
+        w1_q = quantize("w1", w1_bf, H)
+        w3_bf = round_weight("w3", w3_raw, CAST_ENGINES[2], 0)
+        d_sum = reuse.tile([P, PACK, S], F32, name="d_sum", align_bytes=64, offset=4096)
+        y_acc = [product(PACK + t, w1_q, t, x_offs, S) for t in range(PACK)]
+
+        def add_d(t):
+            nc.vector.tensor_tensor(d_sum[:, t, :], d_acc[t][:], d_near[:, t, :], ALU.add)
+
+        add_d(0)
+        for t in range(PACK):
+            evacuate("v", y_win[t][:], y_acc[t], ga_signed[:, t : t + 1])
+            if t > 0:
+                add_d(t)
+
+        w3_q = quantize("w3", w3_bf, H)
+        z_bf = keep.tile([P, PACK * S], BF16, name="z_bf", align_bytes=64)
+        z_dealt = z_bf[:].rearrange("p (u m t) -> p m t u", u=PACK, t=PACK)
+        y_near = keep.tile([P, PACK, FIRST_KEYS], F32, name="y_near")
+        gate = keep.tile([P, PACK, S], F32, name="gate")
+
+        def key_sums(lo, hi):
+            for t in range(PACK):
+                near = y_near[:, t, : hi - lo]
+                nc.scalar.activation(near, y_win[t][:].indirect(l_n1[:, lo // 16 : hi // 16]), ACT.Copy)
+                nc.vector.scalar_tensor_tensor(near, y_acc[t][:, lo:hi], ga_signed[:, t : t + 1], near, ALU.mult, ALU.add)
+
+        def keys(lo, hi):
+            nc.vector.tensor_tensor(
+                z_dealt[:, lo // PACK : hi // PACK],
+                y_near[:, :, : hi - lo].rearrange("p t (m u) -> p m t u", u=PACK),
+                gate[:, :, lo:hi].rearrange("p t (m u) -> p m t u", u=PACK),
+                ALU.mult,
+            )
+
+        b_acc = []
+        for t in range(PACK):
+            b_acc.append(product(t, w3_q, t, x_three, V))
+            evacuate("v", b_win[t][:, :V], b_acc[t], gb_abs[:, t : t + 1])
+        key_sums(0, FIRST_KEYS)
+        nc.scalar.activation(gate[:], d_sum[:], ACT.Sigmoid)
+        keys(0, FIRST_KEYS)
+        b_near = keep.tile([P, PACK, V], F32, name="b_near")
+        b_max = keep.tile([P, PACK, V], F32, name="b_max")
+        for t in range(PACK):
+            fetch(b_near[:, t, :], b_win[t], l_n3)
+            nc.vector.scalar_tensor_tensor(b_max[:, t, :], b_acc[t][:], gb_abs[:, t : t + 1], b_near[:, t, :], ALU.mult, ALU.max)
+        z2_bf = keep.tile([P, PACK * V], BF16, name="z2_bf", align_bytes=64)
+        nc.vector.tensor_copy(
+            z2_bf[:].rearrange("p (c i t) -> p c t i", i=PACK, t=PACK),
+            b_max[:].rearrange("p t (c i) -> p c t i", i=PACK),
+        )
+        z2_q = quantize("z2", z2_bf, V)
+        key_sums(FIRST_KEYS, S)
+        keys(FIRST_KEYS, S)
+        z_q = quantize("z", z_bf, S, pieces=PACK)
+
+        s_acc = []
+        near = keep.tile([P, PACK, 2, V], F32, name="near")
+        for u in range(PACK):
+            s_acc.append(product(u, z_q, u, z2_q, V))
+            nc.vector.tensor_scalar(s_win[u][:, :V], s_acc[u][:], WINDOW_SCALE, None, ALU.mult)
+            fetch(near[:, u, 0, :], s_win[u], l_n4)
+            fetch(near[:, u, 1, :], s_win[u], l_n5)
+        both = keep.tile([P, PACK, V], F32, name="both")
+        qw = keep.tile([P, PACK, 2, V], F32, name="qw")
+        num = keep.tile([P, PACK, V], F32, name="num")
+        squares = keep.tile([P, PACK, 2, V], F32, name="squares")
+        spread = keep.tile([P, PACK, V], F32, name="spread")
+        inv = keep.tile([P, PACK, V], F32, name="inv")
+        res = keep.tile([P, PACK, V], F32, name="res")
+
+        def numerator(u):
+            nc.vector.scalar_tensor_tensor(num[:, u, :], both[:, u, :], N_OF_U, s_acc[u][:], ALU.mult, ALU.subtract)
+
+        for u in range(PACK):
+            nc.vector.tensor_tensor(both[:, u, :], near[:, u, 0, :], near[:, u, 1, :], ALU.add)
+            nc.vector.tensor_tensor(qw[:, u, 1, :], near[:, u, 0, :], near[:, u, 1, :], ALU.subtract)
+            nc.vector.scalar_tensor_tensor(qw[:, u, 0, :], both[:, u, :], Q_OF_U, s_acc[u][:], ALU.mult, ALU.subtract)
+            if u < PACK - 1:
+                numerator(u)
+        numerator(PACK - 1)
+        for u in range(PACK):
+            nc.scalar.activation(squares[:, u], qw[:, u], ACT.Square, scale=SQUARE_SCALE)
+        out_rows = out.rearrange("(p u) v -> p u v", u=PACK)
+        for u in range(PACK):
+            nc.vector.tensor_tensor(spread[:, u, :], squares[:, u, 0, :], squares[:, u, 1, :], ALU.add)
+            nc.scalar.activation(inv[:, u, :], spread[:, u, :], ACT.Abs_reciprocal_sqrt, bias=0.25)
+        for u in range(PACK):
+            nc.vector.scalar_tensor_tensor(res[:, u, :], num[:, u, :], OUT_SCALE, inv[:, u, :], ALU.mult, ALU.mult)
+            nc.sync.dma_start(out_rows[:, u, :], res[:, u, :])

@@ -64,6 +64,10 @@ def tile_picked_twktriebbigstd_none_p_kernel(
         l_two = load_list("l_two", two)
         for q in range(4):
             (nc.scalar if q < 2 else nc.sync).dma_start(x_sc[32 * q : 32 * q + 4, :].bitcast(I32), x_scales[0, 4 * q : 4 * q + 4, :].bitcast(I32))
+        warm_in = keep.tile([P, 1], F32, name="warm_in")
+        nc.vector.memset(warm_in[:], 1.0)
+        warm_out = keep.tile([P, 2], F32, name="warm_out")
+        nc.scalar.activation(warm_out[:, 0:1], warm_in[:], ACT.Sigmoid)
         l_offs = load_list("l_offs", offs)
         x_w = keep.tile([P, T], U32, name="x_w")
         nc.sync.dma_start(x_w[:].bitcast(I32), x_words[0].rearrange("p n t -> p (n t)").bitcast(I32))
@@ -224,6 +228,7 @@ def tile_picked_twktriebbigstd_none_p_kernel(
         )
         z2_q = quantize("z2", z2_bf, V)
         key_sums(FIRST_KEYS, S)
+        nc.scalar.activation(warm_out[:, 1:2], y_near[:, PACK - 1, 0:1], ACT.Abs_reciprocal_sqrt)
         keys(FIRST_KEYS, S)
         z_q = quantize("z", z_bf, S, pieces=PACK)
 

@@ -20,8 +20,8 @@ P = 128
 PACK = 4
 KEY_WINDOW = S + 32
 QUERY_WINDOW = 2 * V
-FIRST_KEYS = 384
-CAST_ENGINES = [["scalar","scalar"],["gpsimd","gpsimd"],["gpsimd","gpsimd"]]
+KEY_EDGES = [0,128,256,384,512]
+CAST_ENGINES = [["scalar","vector"],["vector","vector"],["scalar","vector"]]
 EVAC_D = "ssvv"
 
 WINDOW_SCALE = 1.6
@@ -58,26 +58,28 @@ def tile_picked_twktriebbigstd_none_p_kernel(
 
         x_sc = keep.tile([P, T], U8, name="x_sc")
         nc.vector.memset(x_sc[:].bitcast(I32), 0)
-        w2_all = keep.tile([P, PACK, H], F32, name="w2_raw")
-        nc.sync.dma_start(w2_all[:], w2.rearrange("(p j) c -> p j c", j=PACK))
-        w2_raw = [w2_all[:, :, : H // 2], w2_all[:, :, H // 2 :]]
         l_two = load_list("l_two", two)
+        l_offs = load_list("l_offs", offs)
         for q in range(4):
             (nc.scalar if q < 2 else nc.sync).dma_start(x_sc[32 * q : 32 * q + 4, :].bitcast(I32), x_scales[0, 4 * q : 4 * q + 4, :].bitcast(I32))
         warm_in = keep.tile([P, 1], F32, name="warm_in")
         nc.vector.memset(warm_in[:], 1.0)
         warm_out = keep.tile([P, 2], F32, name="warm_out")
         nc.scalar.activation(warm_out[:, 0:1], warm_in[:], ACT.Sigmoid)
-        l_offs = load_list("l_offs", offs)
         x_w = keep.tile([P, T], U32, name="x_w")
         nc.sync.dma_start(x_w[:].bitcast(I32), x_words[0].rearrange("p n t -> p (n t)").bitcast(I32))
-        w1_raw = [load_half("w1", w1, 0)]
-        l_n2 = load_list("l_n2", n2)
-        w1_raw.append(load_half("w1", w1, 1))
+        w2_all = keep.tile([P, PACK, H], F32, name="w2_raw")
+        nc.sync.dma_start(w2_all[:], w2.rearrange("(p j) c -> p j c", j=PACK))
+        w2_raw = [w2_all[:, :, : 192], w2_all[:, :, 192 :]]
+        w3_raw = [load_half("w3", w3, 0)]
         l_three = load_list("l_three", three)
-        w3_raw = [load_half("w3", w3, 0), load_half("w3", w3, 1)]
-        l_n1 = load_list("l_n1", n1)
+        l_n2 = load_list("l_n2", n2)
+        w3_raw.append(load_half("w3", w3, 1))
+        w1_all = keep.tile([P, PACK, H], F32, name="w1_raw")
+        nc.sync.dma_start(w1_all[:], w1.rearrange("(p j) c -> p j c", j=PACK))
+        w1_raw = [w1_all[:, :, : H // 2], w1_all[:, :, H // 2 :]]
         l_n3 = load_list("l_n3", n3)
+        l_n1 = load_list("l_n1", n1)
         l_n4 = load_list("l_n4", n4)
         l_n5 = load_list("l_n5", n5)
 
@@ -90,7 +92,7 @@ def tile_picked_twktriebbigstd_none_p_kernel(
             return tiles
 
         d_win = windows("d_win", S, KEY_WINDOW)
-        y_win = [keep.tile([P, S], F32, name=f"y_win{t}") for t in range(PACK)]
+        y_win = windows("y_win", S, KEY_WINDOW)
         b_win = windows("b_win", V, QUERY_WINDOW)
         s_win = windows("s_win", V, QUERY_WINDOW)
         ga_sb = load_gain("ga_sb", ga)
@@ -109,23 +111,25 @@ def tile_picked_twktriebbigstd_none_p_kernel(
         def round_weight(name, halves, engines, offset):
             w_bf = reuse.tile([P, PACK * H], BF16, name=f"{name}_bf", align_bytes=64, offset=offset)
             dealt = w_bf[:].rearrange("p (t m j) -> p m j t", t=PACK, j=PACK)
+            lo = 0
             for h, raw in enumerate(halves):
-                dst = dealt[:, h * (P // 2) : (h + 1) * (P // 2)]
+                dst = dealt[:, lo : lo + raw.shape[2] // PACK]
+                lo = lo + raw.shape[2] // PACK
                 src = raw.rearrange("p j (m t) -> p m j t", t=PACK)
                 if engines[h] == "scalar":
                     nc.scalar.copy(dst, src)
                 elif engines[h] == "gpsimd":
                     nc.gpsimd.tensor_scalar(dst.rearrange("p m j t -> p t m j"), src.rearrange("p m j t -> p t m j"), 1.0, 0.0, ALU.mult, ALU.add)
                 else:
-                    nc.vector.tensor_copy(dst, src)
+                    nc.vector.tensor_copy(dst.rearrange("p m j t -> p m t j"), src.rearrange("p m j t -> p m t j"))
             return w_bf
 
-        def quantize(name, bf, words, pieces=1):
+        def quantize(name, bf, words, cuts=()):
             codes = keep.tile([P, words], U32, name=f"{name}_codes", align_bytes=64)
             scales = keep.tile([P, words], U8, name=f"{name}_scales", align_bytes=64)
-            step = words // pieces
-            for c in range(0, words, step):
-                nc.vector.quantize_mx(out=codes[:, c : c + step].bitcast(FP8X4), scales=scales[:, c : c + step], in_=bf[:, PACK * c : PACK * (c + step)])
+            edges = [0, *cuts, words]
+            for lo, hi in zip(edges, edges[1:]):
+                nc.vector.quantize_mx(out=codes[:, lo:hi].bitcast(FP8X4), scales=scales[:, lo:hi], in_=bf[:, PACK * lo : PACK * hi])
             return codes, scales
 
         def product(bank, stationary, t, moving, n):
@@ -153,10 +157,10 @@ def tile_picked_twktriebbigstd_none_p_kernel(
 
         sc_two = pick("two", l_two, S)
         sc_offs = pick("offs", l_offs, S)
-        w2_bf = round_weight("w2", w2_raw, CAST_ENGINES[0], 12288)
-        w2_q = quantize("w2", w2_bf, H)
         x_two = (pick_words("two", l_two, S), sc_two)
         x_offs = (pick_words("offs", l_offs, S), sc_offs)
+        w2_bf = round_weight("w2", w2_raw, CAST_ENGINES[0], 12288)
+        w2_q = quantize("w2", w2_bf, H, [P])
 
         sign = keep.tile([P, PACK], F32, name="sign")
         nc.gpsimd.tensor_scalar(sign[:], gb_sb[:], 0.0, 2.0, ALU.is_ge, ALU.mult)
@@ -165,77 +169,74 @@ def tile_picked_twktriebbigstd_none_p_kernel(
         gb_abs = keep.tile([P, PACK], F32, name="gb_abs")
         nc.gpsimd.tensor_tensor(ga_signed[:], ga_sb[:], sign[:], ALU.mult)
         nc.gpsimd.tensor_tensor(gb_abs[:], gb_sb[:], sign[:], ALU.mult)
-        w1_bf = round_weight("w1", w1_raw, CAST_ENGINES[1], 2048)
+        w3_bf = round_weight("w3", w3_raw, CAST_ENGINES[2], 16384)
 
-        d_acc = []
         d_near = keep.tile([P, PACK, S], F32, name="d_near")
         for t in range(PACK):
-            d_acc.append(product(t, w2_q, t, x_two, S))
-            evacuate(EVAC_D[t], d_win[t][:, :S], d_acc[t], 1.0)
+            d_acc = product(t, w2_q, t, x_two, S)
+            evacuate(EVAC_D[t], d_win[t][:, :S], d_acc, 1.0)
             fetch(d_near[:, t, :], d_win[t], l_n2)
         x_three = (pick_words("three", l_three, V), pick("three", l_three, V))
 
-        w1_q = quantize("w1", w1_bf, H)
-        w3_bf = round_weight("w3", w3_raw, CAST_ENGINES[2], 0)
-        d_sum = reuse.tile([P, PACK, S], F32, name="d_sum", align_bytes=64, offset=4096)
-        y_acc = [product(PACK + t, w1_q, t, x_offs, S) for t in range(PACK)]
-
-        def add_d(t):
-            nc.vector.tensor_tensor(d_sum[:, t, :], d_acc[t][:], d_near[:, t, :], ALU.add)
-
-        add_d(0)
-        for t in range(PACK):
-            evacuate("v", y_win[t][:], y_acc[t], ga_signed[:, t : t + 1])
-            if t > 0:
-                add_d(t)
-
-        w3_q = quantize("w3", w3_bf, H)
-        z_bf = keep.tile([P, PACK * S], BF16, name="z_bf", align_bytes=64)
-        z_dealt = z_bf[:].rearrange("p (u m t) -> p m t u", u=PACK, t=PACK)
-        y_near = keep.tile([P, PACK, FIRST_KEYS], F32, name="y_near")
-        gate = keep.tile([P, PACK, S], F32, name="gate")
-
-        def key_sums(lo, hi):
-            for t in range(PACK):
-                near = y_near[:, t, : hi - lo]
-                nc.scalar.activation(near, y_win[t][:].indirect(l_n1[:, lo // 16 : hi // 16]), ACT.Copy)
-                nc.vector.scalar_tensor_tensor(near, y_acc[t][:, lo:hi], ga_signed[:, t : t + 1], near, ALU.mult, ALU.add)
-
-        def keys(lo, hi):
-            nc.vector.tensor_tensor(
-                z_dealt[:, lo // PACK : hi // PACK],
-                y_near[:, :, : hi - lo].rearrange("p t (m u) -> p m t u", u=PACK),
-                gate[:, :, lo:hi].rearrange("p t (m u) -> p m t u", u=PACK),
-                ALU.mult,
-            )
-
+        w3_q = quantize("w3", w3_bf, H, [P])
+        w1_bf = round_weight("w1", w1_raw, CAST_ENGINES[1], 0)
         b_acc = []
         for t in range(PACK):
-            b_acc.append(product(t, w3_q, t, x_three, V))
+            b_acc.append(product(PACK + t, w3_q, t, x_three, V))
             evacuate("v", b_win[t][:, :V], b_acc[t], gb_abs[:, t : t + 1])
-        key_sums(0, FIRST_KEYS)
-        nc.scalar.activation(gate[:], d_sum[:], ACT.Sigmoid)
-        keys(0, FIRST_KEYS)
+            if t == 0:
+                w1_q = quantize("w1", w1_bf, H, [P])
+        d_sum = reuse.tile([P, PACK, S], F32, name="d_sum", align_bytes=64, offset=0)
+        for t in range(3):
+            nc.gpsimd.tensor_tensor(d_sum[:, t, :], d_win[t][:, :S], d_near[:, t, :], ALU.add)
+        y_acc = []
+        for t in range(PACK - 1):
+            y_acc.append(product(t, w1_q, t, x_offs, S))
+            evacuate("v", y_win[t][:, :S], y_acc[t], ga_signed[:, t : t + 1])
+
         b_near = keep.tile([P, PACK, V], F32, name="b_near")
         b_max = keep.tile([P, PACK, V], F32, name="b_max")
         for t in range(PACK):
             fetch(b_near[:, t, :], b_win[t], l_n3)
             nc.vector.scalar_tensor_tensor(b_max[:, t, :], b_acc[t][:], gb_abs[:, t : t + 1], b_near[:, t, :], ALU.mult, ALU.max)
+            if t == 0:
+                y_acc.append(product(PACK, w1_q, PACK - 1, x_offs, S))
+            if t == 1:
+                evacuate("v", y_win[PACK - 1][:, :S], y_acc[PACK - 1], ga_signed[:, PACK - 1 : PACK])
+        for t in range(3, PACK):
+            nc.vector.tensor_tensor(d_sum[:, t, :], d_acc[:], d_near[:, t, :], ALU.add)
         z2_bf = keep.tile([P, PACK * V], BF16, name="z2_bf", align_bytes=64)
         nc.vector.tensor_copy(
-            z2_bf[:].rearrange("p (c i t) -> p c t i", i=PACK, t=PACK),
-            b_max[:].rearrange("p t (c i) -> p c t i", i=PACK),
+            z2_bf[:].rearrange("p (c t) -> p c t", t=PACK),
+            b_max[:].rearrange("p t c -> p c t"),
         )
         z2_q = quantize("z2", z2_bf, V)
-        key_sums(FIRST_KEYS, S)
-        nc.scalar.activation(warm_out[:, 1:2], y_near[:, PACK - 1, 0:1], ACT.Abs_reciprocal_sqrt)
-        keys(FIRST_KEYS, S)
-        z_q = quantize("z", z_bf, S, pieces=PACK)
+
+        z_bf = keep.tile([P, PACK * S], BF16, name="z_bf", align_bytes=64)
+        z_dealt = z_bf[:].rearrange("p (u m t) -> p m t u", u=PACK, t=PACK)
+        y_near = keep.tile([P, PACK, S], F32, name="y_near")
+        gate = keep.tile([P, PACK, S], F32, name="gate")
+        for t in range(PACK):
+            step = S // 2 if t == PACK - 1 else S
+            for lo in range(0, S, step):
+                near = y_near[:, t, lo : lo + step]
+                nc.scalar.activation(near, y_win[t][:].indirect(l_n1[:, lo // 16 : (lo + step) // 16]), ACT.Copy)
+                nc.vector.scalar_tensor_tensor(near, y_acc[t][:, lo : lo + step], ga_signed[:, t : t + 1], near, ALU.mult, ALU.add)
+        for lo, hi in zip(KEY_EDGES, KEY_EDGES[1:]):
+            nc.scalar.activation(gate[:, :, lo:hi], d_sum[:, :, lo:hi], ACT.Sigmoid)
+            nc.vector.tensor_tensor(
+                z_dealt[:, lo // PACK : hi // PACK],
+                y_near[:, :, lo:hi].rearrange("p t (m u) -> p m t u", u=PACK),
+                gate[:, :, lo:hi].rearrange("p t (m u) -> p m t u", u=PACK),
+                ALU.mult,
+            )
+        nc.scalar.activation(warm_out[:, 1:2], gate[:, PACK - 1, S - 1 : S], ACT.Abs_reciprocal_sqrt)
+        z_q = quantize("z", z_bf, S, cuts=[P, 2 * P, 3 * P])
 
         s_acc = []
         near = keep.tile([P, PACK, 2, V], F32, name="near")
         for u in range(PACK):
-            s_acc.append(product(u, z_q, u, z2_q, V))
+            s_acc.append(product((5, 6, 7, 3)[u], z_q, u, z2_q, V))
             nc.vector.tensor_scalar(s_win[u][:, :V], s_acc[u][:], WINDOW_SCALE, None, ALU.mult)
             fetch(near[:, u, 0, :], s_win[u], l_n4)
             fetch(near[:, u, 1, :], s_win[u], l_n5)

@@ -121,7 +121,7 @@ def tile_picked_twktriebbigstd_none_p_kernel(
                 elif engines[h] == "gpsimd":
                     nc.gpsimd.tensor_scalar(dst.rearrange("p m j t -> p t m j"), src.rearrange("p m j t -> p t m j"), 1.0, 0.0, ALU.mult, ALU.add)
                 else:
-                    nc.vector.tensor_copy(dst.rearrange("p m j t -> p m t j"), src.rearrange("p m j t -> p m t j"))
+                    nc.vector.tensor_copy(dst, src)
             return w_bf
 
         def quantize(name, bf, words, cuts=()):
@@ -207,8 +207,8 @@ def tile_picked_twktriebbigstd_none_p_kernel(
             nc.vector.tensor_tensor(d_sum[:, t, :], d_acc[:], d_near[:, t, :], ALU.add)
         z2_bf = keep.tile([P, PACK * V], BF16, name="z2_bf", align_bytes=64)
         nc.vector.tensor_copy(
-            z2_bf[:].rearrange("p (c t) -> p c t", t=PACK),
-            b_max[:].rearrange("p t c -> p c t"),
+            z2_bf[:].rearrange("p (c i t) -> p c t i", i=PACK, t=PACK),
+            b_max[:].rearrange("p t (c i) -> p c t i", i=PACK),
         )
         z2_q = quantize("z2", z2_bf, V)
 

@@ -18,17 +18,23 @@ ACT = mybir.ActivationFunctionType
 
 P = 128
 PACK = 4
+QUADRANTS = 4
+LIST_ROWS = 16
 KEY_WINDOW = S + 32
 QUERY_WINDOW = 2 * V
-KEY_EDGES = [0,128,256,384,512]
-CAST_ENGINES = [["scalar","vector"],["vector","vector"],["scalar","vector"]]
-EVAC_D = "ssvv"
 
-WINDOW_SCALE = 1.6
-Q_OF_U = 0.375
-N_OF_U = (0.3125 / 25.6) / (0.6875 / 16.0)
-SQUARE_SCALE = 1.0 / (25.6 * math.sqrt(2.0))
-OUT_SCALE = -0.6875 / 16.0
+SCALE_LOADS_ON_SCALAR = 2
+W2_COLUMNS_ON_SCALAR = 192
+D_PLANES_EMPTIED_BY_SCALAR = 2
+D_PLANES_ADDED_BY_GPSIMD = 3
+KEY_PIECE = 128
+
+S_SCALE = 25.6
+WINDOW_OF_RAW = S_SCALE / 16.0
+SPREAD_OF_BOTH = 0.375
+NUMERATOR_OF_BOTH = (0.3125 / S_SCALE) / (0.6875 / 16.0)
+OUT_OF_NUMERATOR = -0.6875 / 16.0
+SQUARE_SCALE = 1.0 / (S_SCALE * math.sqrt(2.0))
 
 
 def tile_picked_twktriebbigstd_none_p_kernel(
@@ -37,108 +43,63 @@ def tile_picked_twktriebbigstd_none_p_kernel(
     nc = tc.nc
     with ExitStack() as ctx:
         keep = ctx.enter_context(tc.tile_pool(name="keep", bufs=1))
-        reuse = ctx.enter_context(tc.tile_pool(name="reuse", bufs=1))
         psum = ctx.enter_context(tc.psum_pool(name="psum", bufs=1))
 
         def load_list(name, src):
-            lst = keep.tile(list(src.shape), U16, name=name)
-            nc.sync.dma_start(lst[:], src)
-            return lst
+            offsets = keep.tile(list(src.shape), U16, name=name)
+            nc.sync.dma_start(offsets[:], src)
+            return offsets
 
-        def load_half(name, w, h):
-            rows = w.rearrange("(p j) c -> p j c", j=PACK)
-            raw = keep.tile([P, PACK, H // 2], F32, name=f"{name}_raw{h}")
-            nc.sync.dma_start(raw[:], rows[:, :, h * (H // 2) : (h + 1) * (H // 2)])
-            return raw[:]
+        def load_weight(name, w, lo, hi):
+            raw = keep.tile([P, PACK, hi - lo], F32, name=name)
+            nc.sync.dma_start(raw[:], w.rearrange("(p j) c -> p j c", j=PACK)[:, :, lo:hi])
+            return raw
 
         def load_gain(name, g):
             gain = keep.tile([P, PACK], F32, name=name)
             nc.gpsimd.dma_start(gain[:], g.rearrange("(p t) o -> p (t o)", t=PACK))
             return gain
 
-        x_sc = keep.tile([P, T], U8, name="x_sc")
-        nc.vector.memset(x_sc[:].bitcast(I32), 0)
-        l_two = load_list("l_two", two)
-        l_offs = load_list("l_offs", offs)
-        for q in range(4):
-            (nc.scalar if q < 2 else nc.sync).dma_start(x_sc[32 * q : 32 * q + 4, :].bitcast(I32), x_scales[0, 4 * q : 4 * q + 4, :].bitcast(I32))
-        warm_in = keep.tile([P, 1], F32, name="warm_in")
-        nc.vector.memset(warm_in[:], 1.0)
-        warm_out = keep.tile([P, 2], F32, name="warm_out")
-        nc.scalar.activation(warm_out[:, 0:1], warm_in[:], ACT.Sigmoid)
-        x_w = keep.tile([P, T], U32, name="x_w")
-        nc.sync.dma_start(x_w[:].bitcast(I32), x_words[0].rearrange("p n t -> p (n t)").bitcast(I32))
-        w2_all = keep.tile([P, PACK, H], F32, name="w2_raw")
-        nc.sync.dma_start(w2_all[:], w2.rearrange("(p j) c -> p j c", j=PACK))
-        w2_raw = [w2_all[:, :, : 192], w2_all[:, :, 192 :]]
-        w3_raw = [load_half("w3", w3, 0)]
-        l_three = load_list("l_three", three)
-        l_n2 = load_list("l_n2", n2)
-        w3_raw.append(load_half("w3", w3, 1))
-        w1_all = keep.tile([P, PACK, H], F32, name="w1_raw")
-        nc.sync.dma_start(w1_all[:], w1.rearrange("(p j) c -> p j c", j=PACK))
-        w1_raw = [w1_all[:, :, : H // 2], w1_all[:, :, H // 2 :]]
-        l_n3 = load_list("l_n3", n3)
-        l_n1 = load_list("l_n1", n1)
-        l_n4 = load_list("l_n4", n4)
-        l_n5 = load_list("l_n5", n5)
-
-        def windows(name, used, width):
+        def windows(name, used, width, engine):
             tiles = []
             for t in range(PACK):
-                win = keep.tile([P, width], F32, name=f"{name}{t}")
-                nc.gpsimd.memset(win[:, used:], 0.0)
-                tiles.append(win)
+                window = keep.tile([P, width], F32, name=f"{name}{t}")
+                engine.memset(window[:, used:], 0.0)
+                tiles.append(window)
             return tiles
 
-        d_win = windows("d_win", S, KEY_WINDOW)
-        y_win = windows("y_win", S, KEY_WINDOW)
-        b_win = windows("b_win", V, QUERY_WINDOW)
-        s_win = windows("s_win", V, QUERY_WINDOW)
-        ga_sb = load_gain("ga_sb", ga)
-        gb_sb = load_gain("gb_sb", gb)
+        def pick(name, table, offsets, count, dtype):
+            picked = keep.tile([P, count], dtype, name=name, align_bytes=64)
+            nc.vector.tensor_copy(picked[:], table[:].indirect(offsets[:]))
+            return picked
 
-        def pick(name, lst, n):
-            sc = keep.tile([P, n], U8, name=f"{name}_sc", align_bytes=64)
-            nc.vector.tensor_copy(sc[:], x_sc[:].indirect(lst[:]))
-            return sc
+        def round_weight(name, shares):
+            rounded = keep.tile([P, PACK * H], BF16, name=name, align_bytes=64)
+            dealt = rounded[:].rearrange("p (t m j) -> p m j t", t=PACK, j=PACK)
+            first = 0
+            for copy, columns in shares:
+                count = columns.shape[2] // PACK
+                copy(dealt[:, first : first + count], columns.rearrange("p j (m t) -> p m j t", t=PACK))
+                first = first + count
+            return rounded
 
-        def pick_words(name, lst, n):
-            wd = keep.tile([P, n], U32, name=f"{name}_w", align_bytes=64)
-            nc.vector.tensor_copy(wd[:], x_w[:].indirect(lst[:]))
-            return wd
-
-        def round_weight(name, halves, engines, offset):
-            w_bf = reuse.tile([P, PACK * H], BF16, name=f"{name}_bf", align_bytes=64, offset=offset)
-            dealt = w_bf[:].rearrange("p (t m j) -> p m j t", t=PACK, j=PACK)
-            lo = 0
-            for h, raw in enumerate(halves):
-                dst = dealt[:, lo : lo + raw.shape[2] // PACK]
-                lo = lo + raw.shape[2] // PACK
-                src = raw.rearrange("p j (m t) -> p m j t", t=PACK)
-                if engines[h] == "scalar":
-                    nc.scalar.copy(dst, src)
-                elif engines[h] == "gpsimd":
-                    nc.gpsimd.tensor_scalar(dst.rearrange("p m j t -> p t m j"), src.rearrange("p m j t -> p t m j"), 1.0, 0.0, ALU.mult, ALU.add)
-                else:
-                    nc.vector.tensor_copy(dst, src)
-            return w_bf
-
-        def quantize(name, bf, words, cuts=()):
+        def quantize(name, rounded, words, cuts):
             codes = keep.tile([P, words], U32, name=f"{name}_codes", align_bytes=64)
             scales = keep.tile([P, words], U8, name=f"{name}_scales", align_bytes=64)
             edges = [0, *cuts, words]
             for lo, hi in zip(edges, edges[1:]):
-                nc.vector.quantize_mx(out=codes[:, lo:hi].bitcast(FP8X4), scales=scales[:, lo:hi], in_=bf[:, PACK * lo : PACK * hi])
+                nc.vector.quantize_mx(
+                    out=codes[:, lo:hi].bitcast(FP8X4), scales=scales[:, lo:hi], in_=rounded[:, PACK * lo : PACK * hi]
+                )
             return codes, scales
 
-        def product(bank, stationary, t, moving, n):
-            acc = psum.tile([P, n], F32, name=f"bank{bank}", tag=f"bank{bank}")
-            cols = slice(t * P, (t + 1) * P)
+        def product(bank, stationary, t, moving, count):
+            acc = psum.tile([P, count], F32, name=f"bank{bank}", tag=f"bank{bank}")
+            columns = slice(t * P, (t + 1) * P)
             nc.tensor.matmul_mx(
                 out=acc[:],
-                lhsT=stationary[0][:, cols].bitcast(FP8X4),
-                lhsT_scale=stationary[1][:, cols],
+                lhsT=stationary[0][:, columns].bitcast(FP8X4),
+                lhsT_scale=stationary[1][:, columns],
                 rhs=moving[0][:].bitcast(FP8X4),
                 rhs_scale=moving[1][:],
                 start=True,
@@ -146,124 +107,188 @@ def tile_picked_twktriebbigstd_none_p_kernel(
             )
             return acc
 
-        def evacuate(engine, dst, acc, scale):
-            if engine == "s":
-                nc.scalar.activation(dst, acc[:], ACT.Copy, scale=scale)
-            else:
-                nc.vector.tensor_scalar(dst, acc[:], scale, None, ALU.mult)
+        def empty_bank(dst, acc, factor):
+            nc.vector.tensor_scalar(dst, acc[:], factor, None, ALU.mult)
 
-        def fetch(dst, win, lst):
-            nc.scalar.activation(dst, win[:].indirect(lst[:]), ACT.Copy)
+        def fetch(dst, window, offsets):
+            nc.scalar.activation(dst, window[:].indirect(offsets), ACT.Copy)
 
-        sc_two = pick("two", l_two, S)
-        sc_offs = pick("offs", l_offs, S)
-        x_two = (pick_words("two", l_two, S), sc_two)
-        x_offs = (pick_words("offs", l_offs, S), sc_offs)
-        w2_bf = round_weight("w2", w2_raw, CAST_ENGINES[0], 12288)
+        x_sc = keep.tile([P, T], U8, name="x_sc")
+        nc.vector.memset(x_sc[:].bitcast(I32), 0)
+        l_two = load_list("l_two", two)
+        l_offs = load_list("l_offs", offs)
+        for q in range(QUADRANTS):
+            queue = nc.scalar if q < SCALE_LOADS_ON_SCALAR else nc.sync
+            queue.dma_start(x_sc[32 * q : 32 * q + 4, :].bitcast(I32), x_scales[0, 4 * q : 4 * q + 4, :].bitcast(I32))
+
+        warm_in = keep.tile([P, 1], F32, name="warm_in")
+        nc.vector.memset(warm_in[:], 1.0)
+        warm_out = keep.tile([P, 2], F32, name="warm_out")
+        nc.scalar.activation(warm_out[:, 0:1], warm_in[:], ACT.Sigmoid)
+
+        x_w = keep.tile([P, T], U32, name="x_w")
+        nc.sync.dma_start(x_w[:].bitcast(I32), x_words[0].rearrange("p n t -> p (n t)").bitcast(I32))
+        w2_raw = load_weight("w2_raw", w2, 0, H)
+        w3_left = load_weight("w3_left", w3, 0, H // 2)
+        l_three = load_list("l_three", three)
+        l_n2 = load_list("l_n2", n2)
+        w3_right = load_weight("w3_right", w3, H // 2, H)
+        w1_raw = load_weight("w1_raw", w1, 0, H)
+        l_n3 = load_list("l_n3", n3)
+        l_n1 = load_list("l_n1", n1)
+        l_n4 = load_list("l_n4", n4)
+        l_n5 = load_list("l_n5", n5)
+        gb_sb = load_gain("gb_sb", gb)
+        ga_sb = load_gain("ga_sb", ga)
+
+        d_win = windows("d_win", S, KEY_WINDOW, nc.vector)
+        y_win = windows("y_win", S, KEY_WINDOW, nc.vector)
+        query_win = windows("query_win", V, QUERY_WINDOW, nc.gpsimd)
+
+        two_sc = pick("two_sc", x_sc, l_two, S, U8)
+        offs_sc = pick("offs_sc", x_sc, l_offs, S, U8)
+        x_two = (pick("two_w", x_w, l_two, S, U32), two_sc)
+        x_offs = (pick("offs_w", x_w, l_offs, S, U32), offs_sc)
+        w2_bf = round_weight(
+            "w2_bf",
+            [
+                (nc.scalar.copy, w2_raw[:, :, :W2_COLUMNS_ON_SCALAR]),
+                (nc.vector.tensor_copy, w2_raw[:, :, W2_COLUMNS_ON_SCALAR:]),
+            ],
+        )
         w2_q = quantize("w2", w2_bf, H, [P])
 
-        sign = keep.tile([P, PACK], F32, name="sign")
-        nc.gpsimd.tensor_scalar(sign[:], gb_sb[:], 0.0, 2.0, ALU.is_ge, ALU.mult)
-        nc.gpsimd.tensor_scalar(sign[:], sign[:], 1.0, -1.0, ALU.mult, ALU.add)
-        ga_signed = keep.tile([P, PACK], F32, name="ga_signed")
         gb_abs = keep.tile([P, PACK], F32, name="gb_abs")
-        nc.gpsimd.tensor_tensor(ga_signed[:], ga_sb[:], sign[:], ALU.mult)
-        nc.gpsimd.tensor_tensor(gb_abs[:], gb_sb[:], sign[:], ALU.mult)
-        w3_bf = round_weight("w3", w3_raw, CAST_ENGINES[2], 16384)
+        nc.scalar.activation(gb_abs[:], gb_sb[:], ACT.Abs)
+        sign_or_zero = keep.tile([P, PACK], F32, name="sign_or_zero")
+        nc.scalar.activation(sign_or_zero[:], gb_sb[:], ACT.Sign)
+        sign = keep.tile([P, PACK], F32, name="sign")
+        nc.scalar.activation(sign[:], sign_or_zero[:], ACT.Sign, bias=0.5)
+        w3_bf = round_weight("w3_bf", [(nc.scalar.copy, w3_left[:]), (nc.vector.tensor_copy, w3_right[:])])
 
         d_near = keep.tile([P, PACK, S], F32, name="d_near")
+        d_acc = []
         for t in range(PACK):
-            d_acc = product(t, w2_q, t, x_two, S)
-            evacuate(EVAC_D[t], d_win[t][:, :S], d_acc, 1.0)
-            fetch(d_near[:, t, :], d_win[t], l_n2)
-        x_three = (pick_words("three", l_three, V), pick("three", l_three, V))
+            d_acc.append(product(t, w2_q, t, x_two, S))
+            if t < D_PLANES_EMPTIED_BY_SCALAR:
+                nc.scalar.activation(d_win[t][:, :S], d_acc[t][:], ACT.Copy, scale=1.0)
+            else:
+                empty_bank(d_win[t][:, :S], d_acc[t], 1.0)
+            fetch(d_near[:, t, :], d_win[t], l_n2[:])
+        x_three = (pick("three_w", x_w, l_three, V, U32), pick("three_sc", x_sc, l_three, V, U8))
 
         w3_q = quantize("w3", w3_bf, H, [P])
-        w1_bf = round_weight("w1", w1_raw, CAST_ENGINES[1], 0)
+        w1_bf = round_weight(
+            "w1_bf", [(nc.vector.tensor_copy, w1_raw[:, :, : H // 2]), (nc.vector.tensor_copy, w1_raw[:, :, H // 2 :])]
+        )
+        ga_signed = keep.tile([P, PACK], F32, name="ga_signed", tag="w1_raw")
+        nc.vector.tensor_tensor(ga_signed[:], ga_sb[:], sign[:], ALU.mult)
         b_acc = []
-        for t in range(PACK):
+
+        def project_b(t):
             b_acc.append(product(PACK + t, w3_q, t, x_three, V))
-            evacuate("v", b_win[t][:, :V], b_acc[t], gb_abs[:, t : t + 1])
-            if t == 0:
-                w1_q = quantize("w1", w1_bf, H, [P])
-        d_sum = reuse.tile([P, PACK, S], F32, name="d_sum", align_bytes=64, offset=0)
-        for t in range(3):
+            empty_bank(query_win[t][:, :V], b_acc[t], gb_abs[:, t : t + 1])
+
+        project_b(0)
+        w1_q = quantize("w1", w1_bf, H, [P])
+        for t in range(1, PACK):
+            project_b(t)
+
+        d_sum = keep.tile([P, PACK, S], F32, name="d_sum", tag="w1_bf", align_bytes=64)
+        for t in range(D_PLANES_ADDED_BY_GPSIMD):
             nc.gpsimd.tensor_tensor(d_sum[:, t, :], d_win[t][:, :S], d_near[:, t, :], ALU.add)
+
+        last = PACK - 1
         y_acc = []
-        for t in range(PACK - 1):
+
+        def empty_y(t):
+            empty_bank(y_win[t][:, :S], y_acc[t], ga_signed[:, t : t + 1])
+
+        for t in range(last):
             y_acc.append(product(t, w1_q, t, x_offs, S))
-            evacuate("v", y_win[t][:, :S], y_acc[t], ga_signed[:, t : t + 1])
+            empty_y(t)
 
         b_near = keep.tile([P, PACK, V], F32, name="b_near")
         b_max = keep.tile([P, PACK, V], F32, name="b_max")
-        for t in range(PACK):
-            fetch(b_near[:, t, :], b_win[t], l_n3)
-            nc.vector.scalar_tensor_tensor(b_max[:, t, :], b_acc[t][:], gb_abs[:, t : t + 1], b_near[:, t, :], ALU.mult, ALU.max)
-            if t == 0:
-                y_acc.append(product(PACK, w1_q, PACK - 1, x_offs, S))
-            if t == 1:
-                evacuate("v", y_win[PACK - 1][:, :S], y_acc[PACK - 1], ga_signed[:, PACK - 1 : PACK])
-        for t in range(3, PACK):
-            nc.vector.tensor_tensor(d_sum[:, t, :], d_acc[:], d_near[:, t, :], ALU.add)
+
+        def larger_b(t):
+            fetch(b_near[:, t, :], query_win[t], l_n3[:])
+            nc.vector.scalar_tensor_tensor(
+                b_max[:, t, :], b_acc[t][:], gb_abs[:, t : t + 1], b_near[:, t, :], ALU.mult, ALU.max
+            )
+
+        larger_b(0)
+        y_acc.append(product(PACK, w1_q, last, x_offs, S))
+        larger_b(1)
+        empty_y(last)
+        for t in range(2, PACK):
+            larger_b(t)
+        for t in range(D_PLANES_ADDED_BY_GPSIMD, PACK):
+            nc.vector.tensor_tensor(d_sum[:, t, :], d_acc[t][:], d_near[:, t, :], ALU.add)
         z2_bf = keep.tile([P, PACK * V], BF16, name="z2_bf", align_bytes=64)
         nc.vector.tensor_copy(
             z2_bf[:].rearrange("p (c i t) -> p c t i", i=PACK, t=PACK),
             b_max[:].rearrange("p t (c i) -> p c t i", i=PACK),
         )
-        z2_q = quantize("z2", z2_bf, V)
+        z2_q = quantize("z2", z2_bf, V, [])
 
         z_bf = keep.tile([P, PACK * S], BF16, name="z_bf", align_bytes=64)
         z_dealt = z_bf[:].rearrange("p (u m t) -> p m t u", u=PACK, t=PACK)
-        y_near = keep.tile([P, PACK, S], F32, name="y_near")
+        y_sum = keep.tile([P, PACK, S], F32, name="y_sum")
         gate = keep.tile([P, PACK, S], F32, name="gate")
         for t in range(PACK):
-            step = S // 2 if t == PACK - 1 else S
+            step = S // 2 if t == last else S
             for lo in range(0, S, step):
-                near = y_near[:, t, lo : lo + step]
-                nc.scalar.activation(near, y_win[t][:].indirect(l_n1[:, lo // 16 : (lo + step) // 16]), ACT.Copy)
-                nc.vector.scalar_tensor_tensor(near, y_acc[t][:, lo : lo + step], ga_signed[:, t : t + 1], near, ALU.mult, ALU.add)
-        for lo, hi in zip(KEY_EDGES, KEY_EDGES[1:]):
+                part = y_sum[:, t, lo : lo + step]
+                fetch(part, y_win[t], l_n1[:, lo // LIST_ROWS : (lo + step) // LIST_ROWS])
+                nc.vector.scalar_tensor_tensor(
+                    part, y_acc[t][:, lo : lo + step], ga_signed[:, t : t + 1], part, ALU.mult, ALU.add
+                )
+        for lo in range(0, S, KEY_PIECE):
+            hi = lo + KEY_PIECE
             nc.scalar.activation(gate[:, :, lo:hi], d_sum[:, :, lo:hi], ACT.Sigmoid)
             nc.vector.tensor_tensor(
                 z_dealt[:, lo // PACK : hi // PACK],
-                y_near[:, :, lo:hi].rearrange("p t (m u) -> p m t u", u=PACK),
+                y_sum[:, :, lo:hi].rearrange("p t (m u) -> p m t u", u=PACK),
                 gate[:, :, lo:hi].rearrange("p t (m u) -> p m t u", u=PACK),
                 ALU.mult,
             )
-        nc.scalar.activation(warm_out[:, 1:2], gate[:, PACK - 1, S - 1 : S], ACT.Abs_reciprocal_sqrt)
-        z_q = quantize("z", z_bf, S, cuts=[P, 2 * P, 3 * P])
+        nc.scalar.activation(warm_out[:, 1:2], gate[:, last, S - 1 : S], ACT.Abs_reciprocal_sqrt)
+        z_q = quantize("z", z_bf, S, [P, 2 * P, 3 * P])
 
+        s_banks = [PACK + 1, PACK + 2, PACK + 3, last]
         s_acc = []
         near = keep.tile([P, PACK, 2, V], F32, name="near")
         for u in range(PACK):
-            s_acc.append(product((5, 6, 7, 3)[u], z_q, u, z2_q, V))
-            nc.vector.tensor_scalar(s_win[u][:, :V], s_acc[u][:], WINDOW_SCALE, None, ALU.mult)
-            fetch(near[:, u, 0, :], s_win[u], l_n4)
-            fetch(near[:, u, 1, :], s_win[u], l_n5)
+            s_acc.append(product(s_banks[u], z_q, u, z2_q, V))
+            empty_bank(query_win[u][:, :V], s_acc[u], WINDOW_OF_RAW)
+            fetch(near[:, u, 0, :], query_win[u], l_n4[:])
+            fetch(near[:, u, 1, :], query_win[u], l_n5[:])
+
         both = keep.tile([P, PACK, V], F32, name="both")
-        qw = keep.tile([P, PACK, 2, V], F32, name="qw")
-        num = keep.tile([P, PACK, V], F32, name="num")
+        spread_diff = keep.tile([P, PACK, 2, V], F32, name="spread_diff")
+        numerator = keep.tile([P, PACK, V], F32, name="numerator")
         squares = keep.tile([P, PACK, 2, V], F32, name="squares")
-        spread = keep.tile([P, PACK, V], F32, name="spread")
-        inv = keep.tile([P, PACK, V], F32, name="inv")
-        res = keep.tile([P, PACK, V], F32, name="res")
-
-        def numerator(u):
-            nc.vector.scalar_tensor_tensor(num[:, u, :], both[:, u, :], N_OF_U, s_acc[u][:], ALU.mult, ALU.subtract)
-
+        square_sum = keep.tile([P, PACK, V], F32, name="square_sum")
+        inverse_root = keep.tile([P, PACK, V], F32, name="inverse_root")
+        result = keep.tile([P, PACK, V], F32, name="result")
         for u in range(PACK):
             nc.vector.tensor_tensor(both[:, u, :], near[:, u, 0, :], near[:, u, 1, :], ALU.add)
-            nc.vector.tensor_tensor(qw[:, u, 1, :], near[:, u, 0, :], near[:, u, 1, :], ALU.subtract)
-            nc.vector.scalar_tensor_tensor(qw[:, u, 0, :], both[:, u, :], Q_OF_U, s_acc[u][:], ALU.mult, ALU.subtract)
-            if u < PACK - 1:
-                numerator(u)
-        numerator(PACK - 1)
+            nc.vector.tensor_tensor(spread_diff[:, u, 1, :], near[:, u, 0, :], near[:, u, 1, :], ALU.subtract)
+            nc.vector.scalar_tensor_tensor(
+                spread_diff[:, u, 0, :], both[:, u, :], SPREAD_OF_BOTH, s_acc[u][:], ALU.mult, ALU.subtract
+            )
+            nc.vector.scalar_tensor_tensor(
+                numerator[:, u, :], both[:, u, :], NUMERATOR_OF_BOTH, s_acc[u][:], ALU.mult, ALU.subtract
+            )
         for u in range(PACK):
-            nc.scalar.activation(squares[:, u], qw[:, u], ACT.Square, scale=SQUARE_SCALE)
+            nc.scalar.activation(squares[:, u], spread_diff[:, u], ACT.Square, scale=SQUARE_SCALE)
+        for u in range(PACK):
+            nc.vector.tensor_tensor(square_sum[:, u, :], squares[:, u, 0, :], squares[:, u, 1, :], ALU.add)
+            nc.scalar.activation(inverse_root[:, u, :], square_sum[:, u, :], ACT.Abs_reciprocal_sqrt, bias=0.25)
         out_rows = out.rearrange("(p u) v -> p u v", u=PACK)
         for u in range(PACK):
-            nc.vector.tensor_tensor(spread[:, u, :], squares[:, u, 0, :], squares[:, u, 1, :], ALU.add)
-            nc.scalar.activation(inv[:, u, :], spread[:, u, :], ACT.Abs_reciprocal_sqrt, bias=0.25)
-        for u in range(PACK):
-            nc.vector.scalar_tensor_tensor(res[:, u, :], num[:, u, :], OUT_SCALE, inv[:, u, :], ALU.mult, ALU.mult)
-            nc.sync.dma_start(out_rows[:, u, :], res[:, u, :])
+            nc.vector.scalar_tensor_tensor(
+                result[:, u, :], numerator[:, u, :], OUT_OF_NUMERATOR, inverse_root[:, u, :], ALU.mult, ALU.mult
+            )
+            nc.sync.dma_start(out_rows[:, u, :], result[:, u, :])

import math
from contextlib import ExitStack

import concourse.mybir as mybir

K, T, S, V, H = 512, 2048, 512, 256, 512
FLOPS = 2 * K * H * (2 * S + V) + 2 * H * S * V

F32 = mybir.dt.float32
BF16 = mybir.dt.bfloat16
I32 = mybir.dt.int32
U32 = mybir.dt.uint32
U16 = mybir.dt.uint16
U8 = mybir.dt.uint8
FP8X4 = mybir.dt.float8_e4m3fn_x4
ALU = mybir.AluOpType
ACT = mybir.ActivationFunctionType

P = 128
PACK = 4
QUADRANTS = 4
LIST_ROWS = 16
KEY_WINDOW = S + 32
QUERY_WINDOW = 2 * V

SCALE_LOADS_ON_SCALAR = 2
W2_COLUMNS_ON_SCALAR = 192
D_PLANES_EMPTIED_BY_SCALAR = 2
D_PLANES_ADDED_BY_GPSIMD = 3
KEY_PIECE = 128

S_SCALE = 25.6
WINDOW_OF_RAW = S_SCALE / 16.0
SPREAD_OF_BOTH = 0.375
NUMERATOR_OF_BOTH = (0.3125 / S_SCALE) / (0.6875 / 16.0)
OUT_OF_NUMERATOR = -0.6875 / 16.0
SQUARE_SCALE = 1.0 / (S_SCALE * math.sqrt(2.0))


def tile_picked_twktriebbigstd_none_p_kernel(
    tc, x_words, x_scales, w1, w2, w3, ga, gb, offs, two, n1, n2, three, n3, n4, n5, out
):
    nc = tc.nc
    with ExitStack() as ctx:
        keep = ctx.enter_context(tc.tile_pool(name="keep", bufs=1))
        psum = ctx.enter_context(tc.psum_pool(name="psum", bufs=1))

        def load_list(name, src):
            offsets = keep.tile(list(src.shape), U16, name=name)
            nc.sync.dma_start(offsets[:], src)
            return offsets

        def load_weight(name, w, lo, hi):
            raw = keep.tile([P, PACK, hi - lo], F32, name=name)
            nc.sync.dma_start(raw[:], w.rearrange("(p j) c -> p j c", j=PACK)[:, :, lo:hi])
            return raw

        def load_gain(name, g):
            gain = keep.tile([P, PACK], F32, name=name)
            nc.gpsimd.dma_start(gain[:], g.rearrange("(p t) o -> p (t o)", t=PACK))
            return gain

        def windows(name, used, width, engine):
            tiles = []
            for t in range(PACK):
                window = keep.tile([P, width], F32, name=f"{name}{t}")
                engine.memset(window[:, used:], 0.0)
                tiles.append(window)
            return tiles

        def pick(name, table, offsets, count, dtype):
            picked = keep.tile([P, count], dtype, name=name, align_bytes=64)
            nc.vector.tensor_copy(picked[:], table[:].indirect(offsets[:]))
            return picked

        def round_weight(name, shares):
            rounded = keep.tile([P, PACK * H], BF16, name=name, align_bytes=64)
            dealt = rounded[:].rearrange("p (t m j) -> p m j t", t=PACK, j=PACK)
            first = 0
            for copy, columns in shares:
                count = columns.shape[2] // PACK
                copy(dealt[:, first : first + count], columns.rearrange("p j (m t) -> p m j t", t=PACK))
                first = first + count
            return rounded

        def quantize(name, rounded, words, cuts):
            codes = keep.tile([P, words], U32, name=f"{name}_codes", align_bytes=64)
            scales = keep.tile([P, words], U8, name=f"{name}_scales", align_bytes=64)
            edges = [0, *cuts, words]
            for lo, hi in zip(edges, edges[1:]):
                nc.vector.quantize_mx(
                    out=codes[:, lo:hi].bitcast(FP8X4), scales=scales[:, lo:hi], in_=rounded[:, PACK * lo : PACK * hi]
                )
            return codes, scales

        def product(bank, stationary, t, moving, count):
            acc = psum.tile([P, count], F32, name=f"bank{bank}", tag=f"bank{bank}")
            columns = slice(t * P, (t + 1) * P)
            nc.tensor.matmul_mx(
                out=acc[:],
                lhsT=stationary[0][:, columns].bitcast(FP8X4),
                lhsT_scale=stationary[1][:, columns],
                rhs=moving[0][:].bitcast(FP8X4),
                rhs_scale=moving[1][:],
                start=True,
                stop=True,
            )
            return acc

        def empty_bank(dst, acc, factor):
            nc.vector.tensor_scalar(dst, acc[:], factor, None, ALU.mult)

        def fetch(dst, window, offsets):
            nc.scalar.activation(dst, window[:].indirect(offsets), ACT.Copy)

        x_sc = keep.tile([P, T], U8, name="x_sc")
        nc.vector.memset(x_sc[:].bitcast(I32), 0)
        l_two = load_list("l_two", two)
        l_offs = load_list("l_offs", offs)
        for q in range(QUADRANTS):
            queue = nc.scalar if q < SCALE_LOADS_ON_SCALAR else nc.sync
            queue.dma_start(x_sc[32 * q : 32 * q + 4, :].bitcast(I32), x_scales[0, 4 * q : 4 * q + 4, :].bitcast(I32))

        warm_in = keep.tile([P, 1], F32, name="warm_in")
        nc.vector.memset(warm_in[:], 1.0)
        warm_out = keep.tile([P, 2], F32, name="warm_out")
        nc.scalar.activation(warm_out[:, 0:1], warm_in[:], ACT.Sigmoid)

        x_w = keep.tile([P, T], U32, name="x_w")
        nc.sync.dma_start(x_w[:].bitcast(I32), x_words[0].rearrange("p n t -> p (n t)").bitcast(I32))
        w2_raw = load_weight("w2_raw", w2, 0, H)
        w3_left = load_weight("w3_left", w3, 0, H // 2)
        l_three = load_list("l_three", three)
        l_n2 = load_list("l_n2", n2)
        w3_right = load_weight("w3_right", w3, H // 2, H)
        w1_raw = load_weight("w1_raw", w1, 0, H)
        l_n3 = load_list("l_n3", n3)
        l_n1 = load_list("l_n1", n1)
        l_n4 = load_list("l_n4", n4)
        l_n5 = load_list("l_n5", n5)
        gb_sb = load_gain("gb_sb", gb)
        ga_sb = load_gain("ga_sb", ga)

        d_win = windows("d_win", S, KEY_WINDOW, nc.vector)
        y_win = windows("y_win", S, KEY_WINDOW, nc.vector)
        query_win = windows("query_win", V, QUERY_WINDOW, nc.gpsimd)

        two_sc = pick("two_sc", x_sc, l_two, S, U8)
        offs_sc = pick("offs_sc", x_sc, l_offs, S, U8)
        x_two = (pick("two_w", x_w, l_two, S, U32), two_sc)
        x_offs = (pick("offs_w", x_w, l_offs, S, U32), offs_sc)
        w2_bf = round_weight(
            "w2_bf",
            [
                (nc.scalar.copy, w2_raw[:, :, :W2_COLUMNS_ON_SCALAR]),
                (nc.vector.tensor_copy, w2_raw[:, :, W2_COLUMNS_ON_SCALAR:]),
            ],
        )
        w2_q = quantize("w2", w2_bf, H, [P])

        gb_abs = keep.tile([P, PACK], F32, name="gb_abs")
        nc.scalar.activation(gb_abs[:], gb_sb[:], ACT.Abs)
        sign_or_zero = keep.tile([P, PACK], F32, name="sign_or_zero")
        nc.scalar.activation(sign_or_zero[:], gb_sb[:], ACT.Sign)
        sign = keep.tile([P, PACK], F32, name="sign")
        nc.scalar.activation(sign[:], sign_or_zero[:], ACT.Sign, bias=0.5)
        w3_bf = round_weight("w3_bf", [(nc.scalar.copy, w3_left[:]), (nc.vector.tensor_copy, w3_right[:])])

        d_near = keep.tile([P, PACK, S], F32, name="d_near")
        d_acc = []
        for t in range(PACK):
            d_acc.append(product(t, w2_q, t, x_two, S))
            if t < D_PLANES_EMPTIED_BY_SCALAR:
                nc.scalar.activation(d_win[t][:, :S], d_acc[t][:], ACT.Copy, scale=1.0)
            else:
                empty_bank(d_win[t][:, :S], d_acc[t], 1.0)
            fetch(d_near[:, t, :], d_win[t], l_n2[:])
        x_three = (pick("three_w", x_w, l_three, V, U32), pick("three_sc", x_sc, l_three, V, U8))

        w3_q = quantize("w3", w3_bf, H, [P])
        w1_bf = round_weight(
            "w1_bf", [(nc.vector.tensor_copy, w1_raw[:, :, : H // 2]), (nc.vector.tensor_copy, w1_raw[:, :, H // 2 :])]
        )
        ga_signed = keep.tile([P, PACK], F32, name="ga_signed", tag="w1_raw")
        nc.vector.tensor_tensor(ga_signed[:], ga_sb[:], sign[:], ALU.mult)
        b_acc = []

        def project_b(t):
            b_acc.append(product(PACK + t, w3_q, t, x_three, V))
            empty_bank(query_win[t][:, :V], b_acc[t], gb_abs[:, t : t + 1])

        project_b(0)
        w1_q = quantize("w1", w1_bf, H, [P])
        for t in range(1, PACK):
            project_b(t)

        d_sum = keep.tile([P, PACK, S], F32, name="d_sum", tag="w1_bf", align_bytes=64)
        for t in range(D_PLANES_ADDED_BY_GPSIMD):
            nc.gpsimd.tensor_tensor(d_sum[:, t, :], d_win[t][:, :S], d_near[:, t, :], ALU.add)

        last = PACK - 1
        y_acc = []

        def empty_y(t):
            empty_bank(y_win[t][:, :S], y_acc[t], ga_signed[:, t : t + 1])

        for t in range(last):
            y_acc.append(product(t, w1_q, t, x_offs, S))
            empty_y(t)

        b_near = keep.tile([P, PACK, V], F32, name="b_near")
        b_max = keep.tile([P, PACK, V], F32, name="b_max")

        def larger_b(t):
            fetch(b_near[:, t, :], query_win[t], l_n3[:])
            nc.vector.scalar_tensor_tensor(
                b_max[:, t, :], b_acc[t][:], gb_abs[:, t : t + 1], b_near[:, t, :], ALU.mult, ALU.max
            )

        larger_b(0)
        y_acc.append(product(PACK, w1_q, last, x_offs, S))
        larger_b(1)
        empty_y(last)
        for t in range(2, PACK):
            larger_b(t)
        for t in range(D_PLANES_ADDED_BY_GPSIMD, PACK):
            nc.vector.tensor_tensor(d_sum[:, t, :], d_acc[t][:], d_near[:, t, :], ALU.add)
        z2_bf = keep.tile([P, PACK * V], BF16, name="z2_bf", align_bytes=64)
        nc.vector.tensor_copy(
            z2_bf[:].rearrange("p (c i t) -> p c t i", i=PACK, t=PACK),
            b_max[:].rearrange("p t (c i) -> p c t i", i=PACK),
        )
        z2_q = quantize("z2", z2_bf, V, [])

        z_bf = keep.tile([P, PACK * S], BF16, name="z_bf", align_bytes=64)
        z_dealt = z_bf[:].rearrange("p (u m t) -> p m t u", u=PACK, t=PACK)
        y_sum = keep.tile([P, PACK, S], F32, name="y_sum")
        gate = keep.tile([P, PACK, S], F32, name="gate")
        for t in range(PACK):
            step = S // 2 if t == last else S
            for lo in range(0, S, step):
                part = y_sum[:, t, lo : lo + step]
                fetch(part, y_win[t], l_n1[:, lo // LIST_ROWS : (lo + step) // LIST_ROWS])
                nc.vector.scalar_tensor_tensor(
                    part, y_acc[t][:, lo : lo + step], ga_signed[:, t : t + 1], part, ALU.mult, ALU.add
                )
        for lo in range(0, S, KEY_PIECE):
            hi = lo + KEY_PIECE
            nc.scalar.activation(gate[:, :, lo:hi], d_sum[:, :, lo:hi], ACT.Sigmoid)
            nc.vector.tensor_tensor(
                z_dealt[:, lo // PACK : hi // PACK],
                y_sum[:, :, lo:hi].rearrange("p t (m u) -> p m t u", u=PACK),
                gate[:, :, lo:hi].rearrange("p t (m u) -> p m t u", u=PACK),
                ALU.mult,
            )
        nc.scalar.activation(warm_out[:, 1:2], gate[:, last, S - 1 : S], ACT.Abs_reciprocal_sqrt)
        z_q = quantize("z", z_bf, S, [P, 2 * P, 3 * P])

        s_banks = [PACK + 1, PACK + 2, PACK + 3, last]
        s_acc = []
        near = keep.tile([P, PACK, 2, V], F32, name="near")
        for u in range(PACK):
            s_acc.append(product(s_banks[u], z_q, u, z2_q, V))
            empty_bank(query_win[u][:, :V], s_acc[u], WINDOW_OF_RAW)
            fetch(near[:, u, 0, :], query_win[u], l_n4[:])
            fetch(near[:, u, 1, :], query_win[u], l_n5[:])

        both = keep.tile([P, PACK, V], F32, name="both")
        spread_diff = keep.tile([P, PACK, 2, V], F32, name="spread_diff")
        numerator = keep.tile([P, PACK, V], F32, name="numerator")
        squares = keep.tile([P, PACK, 2, V], F32, name="squares")
        square_sum = keep.tile([P, PACK, V], F32, name="square_sum")
        inverse_root = keep.tile([P, PACK, V], F32, name="inverse_root")
        result = keep.tile([P, PACK, V], F32, name="result")
        for u in range(PACK):
            nc.vector.tensor_tensor(both[:, u, :], near[:, u, 0, :], near[:, u, 1, :], ALU.add)
            nc.vector.tensor_tensor(spread_diff[:, u, 1, :], near[:, u, 0, :], near[:, u, 1, :], ALU.subtract)
            nc.vector.scalar_tensor_tensor(
                spread_diff[:, u, 0, :], both[:, u, :], SPREAD_OF_BOTH, s_acc[u][:], ALU.mult, ALU.subtract
            )
            nc.vector.scalar_tensor_tensor(
                numerator[:, u, :], both[:, u, :], NUMERATOR_OF_BOTH, s_acc[u][:], ALU.mult, ALU.subtract
            )
        for u in range(PACK):
            nc.scalar.activation(squares[:, u], spread_diff[:, u], ACT.Square, scale=SQUARE_SCALE)
        for u in range(PACK):
            nc.vector.tensor_tensor(square_sum[:, u, :], squares[:, u, 0, :], squares[:, u, 1, :], ALU.add)
            nc.scalar.activation(inverse_root[:, u, :], square_sum[:, u, :], ACT.Abs_reciprocal_sqrt, bias=0.25)
        out_rows = out.rearrange("(p u) v -> p u v", u=PACK)
        for u in range(PACK):
            nc.vector.scalar_tensor_tensor(
                result[:, u, :], numerator[:, u, :], OUT_OF_NUMERATOR, inverse_root[:, u, :], ALU.mult, ALU.mult
            )
            nc.sync.dma_start(out_rows[:, u, :], result[:, u, :])
